import numpy as np, ml_dtypes
CORES = [0,1,2,3]
N = 4
def setup_inputs(rng):
    return {"x": rng.standard_normal((N, 128, 1024), dtype=np.float32).astype(ml_dtypes.bfloat16)}
def reference(x):
    s = x.sum(axis=0, dtype=np.float64).astype(x.dtype)
    return {"y": np.broadcast_to(s, (N,) + s.shape)}

@@ -1,0 +1,45 @@
+from concourse.bass import DstId, RemoteDMATransfer
+
+NR = 4
+ROWS = 128 // NR
+
+SCRATCH = {
+    "xs": ("dram", [NR, 128, 256], "bfloat16"),
+    "land": ("dram", [NR, 128, 256], "bfloat16"),
+    "res": ("dram", [NR, 128, 256], "bfloat16"),
+}
+SEMAPHORES = ["loaded", "left", "arrived", "done", "stored"]
+
+
+def rank_program(g, core, T, topo):
+    rank = T.rank_of(core)
+    reducers = [c for c in range(8) if T.rank_of(c) is None][:NR]
+
+    if rank is not None:
+        g.sync.dma_start(T.xs[:], T.x[:]).then_inc(T.sem.loaded, 16)
+        g.wait_ge(T.sem.loaded, 16)
+        transfers = []
+        for k in range(NR):
+            rid, pid, _se = topo.addr(reducers[k])
+            transfers.append(RemoteDMATransfer(
+                dst_ids=[DstId(rid=rid, pnc=pid)], dma_engine_mask=0xF << (4 * k), remote_sem=T.sem.arrived,
+                src=T.xs[k], dst=T.land[rank]))
+        g.remote_dma_fused(transfers, local_sem=T.sem.left)
+        g.sync.wait_ge(T.sem.done, 16 * NR)
+        g.sync.dma_start(T.y[:], T.res[:]).then_inc(T.sem.stored, 16)
+        g.wait_ge(T.sem.left, 16)
+        g.wait_ge(T.sem.stored, 16)
+        return
+
+    if core in reducers:
+        k = reducers.index(core)
+        g.wait_ge(T.sem.arrived, 4 * NR)
+        ids = []
+        for c in T.cores:
+            rid, pid, _se = topo.addr(c)
+            ids.append(DstId(rid=rid, pnc=pid))
+        g.remote_dma_fused([RemoteDMATransfer(
+            dst_ids=ids, dma_engine_mask=0xFFFF, remote_sem=T.sem.done,
+            srcs=[T.land[r] for r in range(NR)], dsts=[T.res[k] for _c in T.cores], alu_op=1)],
+            local_sem=T.sem.left)
+        g.wait_ge(T.sem.left, 16)

@@ -1,7 +1,6 @@
 from concourse.bass import DstId, RemoteDMATransfer
 
 NR = 4
-ROWS = 128 // NR
 
 SCRATCH = {
     "xs": ("dram", [NR, 128, 256], "bfloat16"),

from concourse.bass import DstId, RemoteDMATransfer

NR = 4

SCRATCH = {
    "xs": ("dram", [NR, 128, 256], "bfloat16"),
    "land": ("dram", [NR, 128, 256], "bfloat16"),
    "res": ("dram", [NR, 128, 256], "bfloat16"),
}
SEMAPHORES = ["loaded", "left", "arrived", "done", "stored"]


def rank_program(g, core, T, topo):
    rank = T.rank_of(core)
    reducers = [c for c in range(8) if T.rank_of(c) is None][:NR]

    if rank is not None:
        g.sync.dma_start(T.xs[:], T.x[:]).then_inc(T.sem.loaded, 16)
        g.wait_ge(T.sem.loaded, 16)
        transfers = []
        for k in range(NR):
            rid, pid, _se = topo.addr(reducers[k])
            transfers.append(RemoteDMATransfer(
                dst_ids=[DstId(rid=rid, pnc=pid)], dma_engine_mask=0xF << (4 * k), remote_sem=T.sem.arrived,
                src=T.xs[k], dst=T.land[rank]))
        g.remote_dma_fused(transfers, local_sem=T.sem.left)
        g.sync.wait_ge(T.sem.done, 16 * NR)
        g.sync.dma_start(T.y[:], T.res[:]).then_inc(T.sem.stored, 16)
        g.wait_ge(T.sem.left, 16)
        g.wait_ge(T.sem.stored, 16)
        return

    if core in reducers:
        k = reducers.index(core)
        g.wait_ge(T.sem.arrived, 4 * NR)
        ids = []
        for c in T.cores:
            rid, pid, _se = topo.addr(c)
            ids.append(DstId(rid=rid, pnc=pid))
        g.remote_dma_fused([RemoteDMATransfer(
            dst_ids=ids, dma_engine_mask=0xFFFF, remote_sem=T.sem.done,
            srcs=[T.land[r] for r in range(NR)], dsts=[T.res[k] for _c in T.cores], alu_op=1)],
            local_sem=T.sem.left)
        g.wait_ge(T.sem.left, 16)
